import numpy as np, ml_dtypes
CORES = [242,247,114,119]
N = 4
BF = ml_dtypes.bfloat16
V, G, H, RO = 1792, 384, 3, 3
W = V + H * G
LIM = 2 ** 19 - 1
def pack(v, p):
    return {"x": np.ascontiguousarray(v.reshape(N, 128, V)).astype(np.int32), "pt": np.ascontiguousarray(p).astype(np.int32)}
def signs(rng, *shape):
    return rng.choice(np.array([-1, 1]), shape)
def points(rng):
    return np.ascontiguousarray(np.argsort(rng.random((N, 8, W)), axis=-1)[..., :V])
def crowd(rng, quiet):
    pool = np.broadcast_to(rng.integers(-2 ** 16, 2 ** 16 + 1, (8, 16, 24)), (N, 8, 16, 24))
    near = np.take_along_axis(pool, rng.integers(0, 24, (N, 8, 1, V)), 3) * rng.choice(np.array([-3, -2, -1, 1, 2, 3]), (N, 8, 1, V))
    noise = np.exp2(2 + 15 * rng.random((N, 8, 1, V))) * rng.standard_normal((N, 8, 16, V), dtype=np.float32)
    loud = near * (rng.random((N, 8, 1, V)) < 0.5) + noise.astype(np.int64)
    dense = rng.choice(np.array([0.15, 0.3, 1.0]), (N, 8, 1, 1))
    calm = rng.integers(-LIM, LIM + 1, (N, 8, 16, V)) * (rng.random((N, 8, 16, V)) < dense)
    v = np.where(rng.random((N, 8, 1, V)) < quiet, calm, loud)
    return np.minimum(np.maximum(v, -LIM), LIM)
def setup_inputs(rng):
    quiet = rng.permuted(np.tile(np.array([0.0, 0.1, 0.3, 0.5, 0.7, 0.9, 0.95, 1.0]), (N, 1)), axis=1).reshape(N, 8, 1, 1)
    rest = rng.permuted(np.tile(np.array([0.0, 0.0, 0.0, 0.0, 0.3, 0.6, 0.8, 0.92]), (N, 1)), axis=1).reshape(N, 8, 1)
    v = crowd(rng, quiet) * (rng.random((N, 8, 1, V)) > 0.03); p = points(rng)
    p = np.where(rng.random((N, 8, V)) < rest, np.arange(V), p)
    o = np.argsort(rng.random((N, 8, V)), axis=-1); t = V // 16; i = o[..., :t]; s = o[..., t:2 * t]
    np.put_along_axis(v, i[:, :, None, :], np.take_along_axis(v, s[:, :, None, :], 3) * signs(rng, N, 8, 1, t), 3)
    np.put_along_axis(p, i, s, 2)
    return pack(v, p)
def setup_inputs_room(rng):
    v = signs(rng, N, 8, 16, V) * rng.integers(4, 1001, (N, 8, 16, V)); p = np.zeros((N, 8, V), np.int64)
    for q in range(N):
        for g in range(8):
            o = rng.permutation(V); a, b, z, m = o[:32], o[32:64], o[64:320], o[320:]
            v[q, g][:, b] = signs(rng, 16, 32) * rng.integers(5000, LIM + 1, (16, 32))
            v[q, g][:, o[64:320]] = 0; v[q, g][:, a] = 0
            v[q, g][rng.integers(0, 16, 32), a] = signs(rng, 32) * rng.integers(1, 4, 32)
            u = rng.random(V)
            w = np.where(u < 0.5, z[rng.integers(0, 256, V)], np.where(u < 0.75, b[rng.integers(0, 32, V)], np.arange(V)))
            w[b] = np.where(rng.random(32) < 0.5, b, z[rng.integers(0, 256, 32)])
            w[z] = rng.integers(V, W, 256)
            w[z[:H]] = V + np.arange(H) * G + G - 1; w[z[H:2 * H]] = V + np.arange(H) * G; w[a[:2 * H]] = z[:2 * H]
            n = int(rng.choice(np.array([0, 1, G - 1, G, G + 1, V - 320])))
            if q == 0: n = (G, G + 1, V - 320, G - 1, 1, 0, G, G + 1)[g]
            w[rng.permutation(m)[:n]] = a[rng.integers(0, 32, n)]
            p[q, g] = w
    return pack(v, p)
def setup_inputs_ties(rng):
    v = np.zeros((N, 8, 16, V), np.int64); p = np.zeros((N, 8, V), np.int64); h = (V - 2) // 2
    alt = np.where(np.arange(16) % 2 == 0, 1, -1)[:, None]
    for q in range(N):
        for g in range(8):
            o = rng.permutation(V); s, i = o[2:2 + h], o[2 + h:2 + 2 * h]
            y = np.repeat(2 * np.exp2(17 * rng.random((8, h))).astype(np.int64), 2, axis=0) * signs(rng, 16, h)
            one = np.zeros((16, h), np.int64); one[rng.integers(0, 16, h), np.arange(h)] = signs(rng, h)
            big = signs(rng, 16, h) * rng.integers(1, LIM + 1, (16, h)); sg = signs(rng, h); k = rng.integers(0, 7, h)
            kinds = np.stack([y * sg, (y >> 1) * sg, y * sg + one, y * alt * sg, big, 0 * y, big])
            v[q, g, int(rng.integers(0, 16)), o[0]] = 1
            v[q, g][:, s] = y; v[q, g][:, i] = kinds[k, :, np.arange(h)].T
            p[q, g, o[:2]] = rng.integers(0, W, 2)
            p[q, g, s] = rng.integers(0, W, h) if g % 2 == 0 else rng.choice(np.array([0, V - 1, V, W - 1]), h)
            p[q, g, i] = np.where(k == 4, o[0], np.where(k == 6, o[1], s))
    return pack(v, p)
def setup_inputs_still(rng):
    v = crowd(rng, np.zeros((N, 8, 1, 1)))
    lone = np.where(np.arange(16)[:, None] == rng.integers(0, 16, (N, 8, 1, V)), rng.integers(1, LIM + 1, (1, 8, 1, 1)) * signs(rng, N, 8, 1, V), 0)
    mask = np.zeros((N, 8, 1, 1), bool); q = int(rng.integers(0, N)); mask[q] = True; mask[:, int(rng.integers(0, 8))] = True
    own = np.argsort(rng.random((N, 8, V)), axis=-1)
    p = np.where(rng.random((N, 8, V)) < 0.5, rng.integers(V, W, (N, 8, V)), own); p[q] = own[q]
    return pack(np.where(mask, lone, v), p)
def setup_inputs_spread(rng):
    v = (np.exp2(19 * rng.random((N, 8, 1, V))) * np.exp2(-4 * rng.random((N, 8, 16, 1))) * (2 * rng.random((N, 8, 16, V)) - 1)).astype(np.int64)
    v = np.where(rng.random((N, 8, 1, V)) < 0.05, LIM * signs(rng, N, 8, 16, V), v) * (rng.random((N, 8, 1, V)) > 0.0625)
    p = points(rng); odd = (np.arange(8) % 2 == 1)[None, :, None]
    few = np.minimum((W * rng.random((N, 8, V)) ** 4).astype(np.int64), W - 1); few = np.where(rng.random((N, 8, V)) < 0.5, few, W - 1 - few)
    return pack(v, np.where(odd, few, p))
def small(rng, n):
    return signs(rng, 16, n) * rng.integers(1, 1001, (16, n))
def long(rng, n):
    return signs(rng, 16, n) * rng.integers(5000, LIM - 999, (16, n))
def stops(rng, v, p, red):
    o = rng.permutation(np.setdiff1d(np.arange(V), red)); y, w, z = o[:24], o[24:48], o[48:120].reshape(3, 24)
    base = long(rng, 24); i = np.concatenate([rng.integers(0, 24, len(red)), np.arange(24)]); m = np.concatenate([red, w])
    v[:, y] = base; v[:, m] = base[:, i] * signs(rng, len(m)) + small(rng, len(m))
    p[y] = y; p[red] = y[i[:len(red)]]; p[w] = z[0]; p[z[0]] = z[1]; p[z[1]] = z[2]; p[z[2]] = y
def far(rng, v, p):
    base = long(rng, 24); kk = rng.integers(0, 24, (N, G)); at = rng.integers(V, W, (N, V))
    kind = kk[(np.arange(N)[:, None] - (at - V) // G - 1) % N, (at - V) % G]
    for q in range(N):
        v[q] = base[:, kind[q]] * signs(rng, V) + small(rng, V)
        v[q][:, :G] = base[:, kk[q]] * signs(rng, G)
        p[q] = at[q]
def one(rng, v, p):
    base = long(rng, 1); j = rng.integers(0, G, N); turn = int(rng.integers(0, 2))
    for q in range(N):
        d = int(rng.integers(1, H + 1))
        v[q] = base * signs(rng, V) + small(rng, V)
        v[q][:, j[q]] = base[:, 0] * int(signs(rng, 1)[0])
        p[q] = j[q] if (q + turn) % 2 == 0 else V + (d - 1) * G + j[(q - d) % N]
        p[q, j[q]] = j[q]
def grow(rng, v, p):
    o = rng.permutation(16); u = int(rng.integers(480000, LIM - 199)); form = np.zeros((16, 3), np.int64)
    form[o[0]] = (u, u, 3 * u // 4); form[o[1:4]] = (-u, u, -(u // 2)); form[o[4:]] = (u, -(u // 3), 0)
    for q in range(N):
        m = rng.permutation(V); y, s, x, w, z = m[:24], m[24:48], m[48:120], m[120:168], m[168:312].reshape(3, 48)
        for k, i in ((0, x), (0, w), (1, y), (2, s)):
            v[q][:, i] = (form[:, k:k + 1] + rng.integers(-200, 201, (16, len(i)))) * signs(rng, len(i))
        p[q, x] = y[rng.integers(0, 24, 72)]; p[q, y] = s[rng.integers(0, 24, 24)]; p[q, s] = s
        p[q, w] = z[0]; p[q, z[0]] = z[1]; p[q, z[1]] = z[2]; p[q, z[2]] = V + rng.integers(0, H, 48) * G + rng.integers(0, 96, 48)
def setup_inputs_full(rng):
    v = np.zeros((N, 8, 16, V), np.int64); p = points(rng); kind = rng.permutation(np.array([0, 1, 2, 3, 4, 0, 1, 4]))
    for g in range(8):
        if kind[g] == 2: far(rng, v[:, g], p[:, g])
        elif kind[g] == 3: one(rng, v[:, g], p[:, g])
        elif kind[g] == 4: grow(rng, v[:, g], p[:, g])
        else:
            for q in range(N):
                red = np.arange(int(rng.integers(0, 16)), V, 16) if kind[g] == 0 else 256 * int(rng.integers(1, V // 256)) + np.arange(256)
                stops(rng, v[q, g], p[q, g], red)
    return pack(v, p)
def check_inputs(d):
    bad = []
    for k, lo, hi in (("x", -LIM, LIM), ("pt", 0, W - 1)):
        if np.min(d[k]) < lo or np.max(d[k]) > hi: bad.append("range of " + k)
    return bad
def reference(x, pt):
    v = x.astype(np.int64).reshape(N, 8, 16, V); p = pt.astype(np.int64)
    num = np.broadcast_to(np.arange(G), (N, 8, G)); gv = v[..., :G]
    for rnd in range(RO):
        w = np.concatenate([v] + [np.roll(gv, d, axis=0) for d in range(1, H + 1)], axis=3)
        ptr = np.concatenate([p] + [np.roll(num, d, axis=0) for d in range(1, H + 1)], axis=2)
        y = np.take_along_axis(w, p[:, :, None, :], 3)
        old = np.sum(np.abs(v), axis=2); lp = np.sum(np.abs(v + y), axis=2); lm = np.sum(np.abs(v - y), axis=2)
        plus = (lp > 0) & (lp < old); minus = (lm > 0) & (lm < old)
        v = np.where(plus[:, :, None, :], v + y, np.where(minus[:, :, None, :], v - y, v))
        done = plus | minus
        p = np.where(done, p, np.take_along_axis(ptr, p, 2))
        num = np.argsort(np.where(done, 0, 1), axis=2, kind="stable")[..., :G]
        gv = np.take_along_axis(v, num[:, :, None, :], 3)
    return {"yx": v.reshape(N, 128, V).astype(np.float32), "yc": p.astype(np.float32)}

from concourse.bass import DstId, RemoteDMATransfer
from concourse.mybir import AluOpType, ActivationFunctionType

V, G, H, RO = 1792, 384, 3, 3
W = V + H * G
NC = V // 16
CH = V // 4
XO = 2 * V
K0 = 16 * 136
BIG = float(2 ** 20)
SPARE = 2304
STEP = 2560
ZW = STEP + V + 8
NS = 144

F32, BF, I32, U16 = "float32", "bfloat16", "int32", "uint16"
SCRATCH = {"b0": ("sbuf", [128, XO + V], F32), "xi": ("sbuf", [128, W], I32), "pw3": ("sbuf", [128, V], BF),
           "pb": ("sbuf", [128, NC], I32), "ci": ("sbuf", [128, 4], I32)}
for _names, _cols, _dt in (
        ("b1 b2", XO + W, F32), ("xo xc absp absm", V, F32), ("pw0 pw1 pw2", W, BF), ("zw0 zw1", ZW, F32),
        ("gb0 gb1 iot", G, F32), ("hm0 hm1", G, BF), ("phi plo ra rb", NC, BF),
        ("pk vws pwf pws tt qt qq ycb", NC, F32), ("cf b16", 16, F32), ("m16 base pc rst sc", 2 * NS, F32),
        ("zi zv", NS, F32), ("u", NS, BF), ("ident ov", 128, F32), ("blk lt", 128, BF), ("rm ev", 2 * NS, BF),
        ("old f1 ot ou", 256, F32), ("f", 256, BF), ("og uo qo", NC, U16), ("so ho", 32, U16)):
    for _n in _names.split():
        SCRATCH[_n] = ("sbuf", [128, _cols], _dt)
for _k in range(8):
    SCRATCH["k%d" % _k] = ("psum", [128, 512], F32)
SEMAPHORES = ["cv", "cs", "ct", "cg", "sent", "ar0", "ar1", "ar2", "ah1", "ah2"] + ["d%d" % i for i in range(12)]

A = AluOpType
FN = ActivationFunctionType


def rank_program(g, core, T, topo):
    rank = T.rank_of(core)
    if rank is None:
        return
    cores = list(T.cores)
    n = len(cores)
    Q = {"g": g, "v": g.vector, "s": g.scalar, "t": g.tensor, "y": g.sync}
    total = {}
    waited = {}
    wr = {}
    rd = {}
    bank = {}
    ndma = [0]

    def before(e, R, Wr, B):
        toks = []
        for r in R:
            if r in wr:
                toks.append(wr[r])
        for r in Wr:
            if r in wr:
                toks.append(wr[r])
            toks += rd.get(r, [])
        for b in B:
            toks += [t for q, t in bank.get(b, {}).items() if q != e]
        top = {}
        for s, c, q in toks:
            if not (q == "t" and e == "t"):
                top[s] = max(top.get(s, 0), c)
        for s, c in top.items():
            if waited.get((e, s), 0) < c:
                Q[e].wait_ge(T.sem[s], c)
                waited[(e, s)] = c

    def after(e, tok, R, Wr, B):
        for r in R:
            rd.setdefault(r, []).append(tok)
        for r in Wr:
            wr[r] = tok
            rd[r] = []
        for b in B:
            bank.setdefault(b, {})[e] = tok

    def op(e, call, R=(), Wr=(), B=()):
        before(e, R, Wr, B)
        s = "c" + e
        call(Q[e]).then_inc(T.sem[s], 1)
        total[s] = total.get(s, 0) + 1
        after(e, (s, total[s], e), R, Wr, B)

    def dma(e, out, in_, R=(), Wr=()):
        before(e, R, Wr, ())
        s = "d%d" % ndma[0]
        ndma[0] += 1
        Q[e].dma_start(out, in_).then_inc(T.sem[s], 16)
        total[s] = 16
        after(e, (s, 16, "dma"), R, Wr, ())

    def masks(src):
        others = [c for c in cores if c != src]
        far = [c for c in others if c not in topo.cores_of(src)]
        near = [c for c in others if c in topo.cores_of(src)]
        res = {}
        used = set()
        for i, c in enumerate(far):
            en = topo.engines(src, c)
            k = len(en) // len(far)
            res[c] = en[i * k:(i + 1) * k]
            used |= set(en)
        for i, c in enumerate(near):
            en = [x for x in topo.engines(src, c) if x not in used]
            k = len(en) // len(near)
            res[c] = en[i * k:(i + 1) * k]
        return res

    mine = masks(core)
    landing = sum(len(masks(c)[core]) for c in cores if c != core)

    def spread(src, buf, first, sem, R, region):
        before("g", R, (), ())
        trs = []
        for c, en in mine.items():
            d = (T.rank_of(c) - rank) % n
            rid, pid = topo.addr(c, core)
            at = first + (d - 1) * G
            trs.append(RemoteDMATransfer(dst_ids=[DstId(rid=rid, pnc=pid)], dma_engine_mask=sum(1 << x for x in en),
                                         remote_sem=T.sem[sem], src=src, dst=buf[:, at:at + G]))
        g.remote_dma_fused(trs, local_sem=T.sem.sent)
        total["sent"] = total.get("sent", 0) + sum(len(en) for en in mine.values())
        total[sem] = landing
        wr[region] = (sem, landing, "far")

    def ts(out, in0, s1, s2, o0, o1, R, Wr, B=()):
        if o1 is None:
            op("v", lambda q: q.tensor_scalar(out, in0, s1, None, o0), R, Wr, B)
        else:
            op("v", lambda q: q.tensor_scalar(out, in0, s1, s2, o0, o1), R, Wr, B)

    def tt(out, a, b, o, R, Wr, B=()):
        op("v", lambda q: q.tensor_tensor(out, a, b, o), R, Wr, B)

    def cp(out, a, R, Wr, B=()):
        op("v", lambda q: q.tensor_copy(out, a), R, Wr, B)

    def fill(ap, val, Wr):
        op("v", lambda q: q.memset(ap, val), (), Wr)

    def act(out, a, fn, R, Wr, B=(), bias=0.0, scale=1.0):
        op("s", lambda q: q.activation(out, a, fn, bias=bias, scale=scale), R, Wr, B)

    def move(e, out, a, R, Wr):
        if e == "v":
            cp(out, a, R, Wr)
        else:
            op("s", lambda q: q.activation(out, a, FN.Identity), R, Wr)

    def mm(out, lhsT, rhs, st, sp, R, B):
        op("t", lambda q: q.matmul(out, lhsT, rhs, st, sp), R, (), [B])

    def iota(out, pat, base, cm, Wr, flt=True):
        if flt:
            op("g", lambda q: q.iota(out, pat, base, cm, allow_small_or_imprecise_dtypes=True), (), Wr)
        else:
            op("g", lambda q: q.iota(out, pat, base, cm), (), Wr)

    def sel(out, in_, pat, cmp, fl, base, cm, R, Wr):
        op("g", lambda q: q.affine_select(out, in_, pat, cmp, fl, base, cm), R, Wr)

    bufs = [T.b0, T.b1, T.b2]
    pws = [T.pw0, T.pw1, T.pw2, T.pw3]
    X2 = [T.k0, T.k1, T.k2, T.k3]
    L, S1, PB, ZB = T.k4, T.k5, T.k6, T.k7
    cf = T.cf
    E = [T.u[:, 15 - l:143 - l] for l in range(16)]
    LANE, PART, G15, G16, HOME, UPD, ZC, VW = [cf[:, j:j + 1] for j in range(8)]

    pieces = [(0, G), (G, 1088), (1088, V)]
    xin = ["xi%d" % j for j in range(3)]
    dma("y", T.xi[:, 0:G], T.x[:, 0:G], (), ["xi0"])
    dma("s", T.pb[:], T.pt[:], (), ["pb"])
    for j in (1, 2):
        a, b = pieces[j]
        dma("y", T.xi[:, a:b], T.x[:, a:b], (), [xin[j]])

    iota(T.ci[:, 0:1], [[0, 1]], 0, 1, ["ci0"], False)
    iota(T.iot[:], [[1, G]], 0, 0, ["iot"])
    iota(T.m16[:], [[0, 9], [1, 16], [0, 2]], 0, 0, ["m16"])
    spread(T.xi[:, 0:G], T.xi, V, "ar0", ["xi0"], "g0")

    fill(T.pw0[:, 0:V], 0.0, ["p0a", "p0b"])
    ts(T.ci[:, 1:2], T.ci[:, 0:1], 15, None, A.bitwise_and, None, ["ci0"], ["ci1"])
    cp(PART, T.ci[:, 0:1], ["ci0"], ["part"])
    cp(LANE, T.ci[:, 1:2], ["ci1"], ["lane"])
    fill(T.rm[:, 0:288:2], 1.0, ["rm0", "rm1", "rm4"])
    ts(HOME, LANE, -1.0 / 16, 136 + 7.5 / 16, A.mult, A.add, ["lane"], ["home"])
    ts(ZC, LANE, -2.0, 64.0 * 136 + 31, A.mult, A.add, ["lane"], ["zc"])
    ts(VW, LANE, 2.0 ** -12, None, A.mult, None, ["lane"], ["vw"])
    ts(G15, PART, LANE, 15.0, A.subtract, A.add, ["lane", "part"], ["g15"])
    ts(G16, PART, LANE, None, A.subtract, None, ["lane", "part"], ["g16"])
    ts(UPD, LANE, float(XO), None, A.add, None, ["lane"], ["upd"])
    fill(T.rm[:, 1:224:2], -4096.0, ["rm2"])
    fill(T.rm[:, 225:272:2], 4096.0, ["rm3"])
    fill(T.rm[:, 273:288:2], 0.0, ["rm5"])
    fill(T.blk[:], 1.0, ["blk"])
    fill(T.lt[:], 2.0 ** -11, ["lt"])
    ts(T.u[:], T.iot[:, 0:NS], G15, None, A.is_equal, None, ["iot", "g15"], ["u"])
    ts(T.pk[:], T.pb[:], float(K0), None, A.add, None, ["pb"], ["pk"])
    cp(T.phi[:], T.pk[:], ["pk"], ["phi"])
    tt(T.plo[:], T.pk[:], T.phi[:], A.subtract, ["pk", "phi"], ["plo"])
    dma("y", T.pw0[0:128:16, 0:V], T.phi[:], ["phi"], ["p0a"])
    dma("y", T.pw0[1:128:16, 0:V], T.plo[:], ["plo"], ["p0b"])

    for d in range(H):
        act(T.pw0[:, V + d * G:V + (d + 1) * G], T.iot[:], FN.Identity, ["iot", "home"], ["h0_%d" % d], bias=HOME, scale=1.0 / 16)
    act(T.base[:, 0:288:2], T.iot[:, 0:NS], FN.Identity, ["iot"], ["base0"], bias=BIG, scale=0.0)
    act(T.base[:, 1:288:2], T.iot[:, 0:NS], FN.Identity, ["iot"], ["base1"], bias=BIG + SPARE)
    act(T.zi[:, 0:NC], T.iot[:, 0:NC], FN.Identity, ["iot"], ["zi0"], bias=64.0 * 136 + 33, scale=64.0)
    act(T.zi[:, NC:136], T.iot[:, 0:24], FN.Identity, ["iot", "zc"], ["zi1"], bias=ZC, scale=64.0)
    act(T.zi[:, 136:NS], T.iot[:, 0:8], FN.Identity, ["iot"], ["zi2"], bias=-64000.0, scale=0.0)
    act(T.base[:, 224:272:2], T.iot[:, 0:24], FN.Identity, ["iot"], ["base0"], bias=BIG, scale=16.0)
    act(T.base[:, 225:272:2], T.iot[:, NC:136], FN.Identity, ["iot"], ["base1"], bias=BIG + SPARE - 65536)
    act(T.base[:, 272:273], T.iot[:, 0:1], FN.Identity, ["iot"], ["base0"], bias=BIG + STEP)
    act(T.vws[:], T.iot[:, 0:NC], FN.Identity, ["iot", "vw"], ["vws"], bias=VW, scale=2.0 ** -8)
    for r, z in enumerate((T.zw0, T.zw1)):
        act(z[:, STEP:STEP + G], T.iot[:], FN.Identity, ["iot"], ["zs%d" % r], bias=1.0 / 32, scale=0.0)

    for j in range(2):
        ts(T.b16[:, 8 * j:8 * j + 8], T.iot[:, 0:128:16], G16, None, A.is_equal, None, ["iot", "g16"], ["b16_%d" % j])
    ts(T.ident[:], T.iot[:, 0:128], PART, None, A.is_equal, None, ["iot", "part"], ["ident"])
    cp(T.b0[:, XO:XO + G], T.xi[:, 0:G], ["xi0"], ["x0_0"])
    fill(T.f[96:128, :], 1.0, ["f"])
    fill(T.rst[:], 4.0 * BIG, ["rst"])
    ts(T.pc[:], T.m16[:], LANE, None, A.is_equal, None, ["m16", "lane"], ["pc"])
    fill(T.rst[:, 0:288:32], 0.0, ["rst"])
    tt(T.pc[:], T.pc[:], T.base[:], A.mult, ["pc", "base0", "base1"], ["pc"])
    for j in (1, 2):
        a, b = pieces[j]
        cp(T.b0[:, XO + a:XO + b], T.xi[:, a:b], [xin[j]], ["x0_%d" % j])

    sel(T.rm[:, 0:224:2], T.rm[:, 0:224:2], [[1, NC]], A.is_gt, 0.0, 0, -1, ["rm0"], ["rm0"])
    sel(T.rm[:, 224:272:2], T.rm[:, 224:272:2], [[-1, 24]], A.is_ge, 0.0, 0, 1, ["rm1"], ["rm1"])
    sel(T.rm[:, 1:224:2], T.rm[:, 1:224:2], [[1, NC]], A.is_equal, 0.0, 0, -1, ["rm2"], ["rm2"])
    sel(T.rm[:, 225:272:2], T.rm[:, 225:272:2], [[1, 24]], A.is_equal, 0.0, 0, -1, ["rm3"], ["rm3"])
    iota(T.ra[:], [[16, NC]], 0, 0, ["ra"])
    sel(T.blk[:], T.blk[:], [[-16, 8], [0, 16]], A.is_ge, 0.0, 0, 1, ["blk"], ["blk"])
    sel(T.ra[:], T.ra[:], [[0, NC]], A.is_equal, 0.0, -NC, 1, ["ra"], ["ra"])
    sel(T.blk[:], T.blk[:], [[16, 8], [0, 16]], A.is_ge, 0.0, 15, -1, ["blk"], ["blk"])
    sel(T.rb[:], T.ra[:], [[-1, NC]], A.not_equal, float(-V), 0, 1, ["ra"], ["rb"])
    sel(T.lt[:], T.lt[:], [[1, 128]], A.is_ge, 0.0, 0, -1, ["lt"], ["lt"])
    sel(T.ra[:], T.ra[:], [[-1, NC]], A.not_equal, float(-XO), 0, 1, ["ra"], ["ra"])
    sel(T.lt[:], T.lt[:], [[-16, 8], [0, 16]], A.is_ge, 0.0, 0, 1, ["lt"], ["lt"])
    for r, z in enumerate((T.zw0, T.zw1)):
        iota(z[:, 0:G], [[0, G]], -10000, 0, ["zz%d" % r])
    RM = ["rm%d" % j for j in range(6)]

    allm = ["am0", "am1", "am2", "am3a", "am3b"]
    for j in range(3):
        a, b = pieces[j]
        act(T.absm[:, a:b], T.b0[:, XO + a:XO + b], FN.Abs, ["x0_%d" % j], ["ax%d" % j])

    def twice(r, xr):
        for a in range(4):
            act(X2[a][:, 0:CH], bufs[r][:, XO + a:XO + V:4], FN.Identity, xr, (), ["k%d" % a], scale=2.0)

    def offsets(r, pr):
        pw = pws[r]
        for h, (bk, nm) in enumerate(((S1, "k5"), (ZB, "k7"))):
            for a in (2 * h, 2 * h + 1):
                for e in range(16):
                    mm(bk[:, 28 * (a % 2):28 * (a % 2) + 28], E[e], pw[:, 4 * e + a:V:64], e == 0, e == 15, pr + ["u"], nm)
            ts(T.og[:, 56 * h:56 * h + 56], bk[:, 0:56], float(-K0), None, A.add, None, (), ["og%d" % h], [nm])
        for e in range(16):
            mm(PB[:, 0:NC], E[e], pw[:, e:V:16], e == 0, e == 15, pr + ["u"], "k6")

    x0r = ["x0_0", "x0_1", "x0_2"]
    offsets(0, ["p0a", "p0b"])
    twice(0, x0r)
    for l in range(16):
        mm(L[0:NC, l:256:16], T.absm[:, l:V:16], T.b16[:], True, True, ["ax0", "ax1", "ax2", "b16_0", "b16_1"] + allm, "k4")

    xr = x0r
    pr = ["p0a", "p0b", "h0_0", "h0_1", "h0_2"]
    for r in range(RO):
        last = r == RO - 1
        buf = bufs[r]
        if r == 0:
            act(T.old[0:NC, :], L[0:NC, 0:256], FN.Identity, (), ["olda", "oldb"], ["k4"])
        act(T.pwf[:], PB[:, 0:NC], FN.Identity, (), ["pwf"], ["k6"], bias=float(-K0))
        act(T.pws[:], PB[:, 0:NC], FN.Identity, (), ["pws"], ["k6"], bias=-K0 * 2.0 ** -12, scale=2.0 ** -12)
        if not last:
            mm(PB[:, 0:288], T.ident[:], T.pc[:], True, False, ["ident", "pc"], "k6")
            mm(ZB[:, 0:NS], T.ident[:], T.zi[:], True, False, ["ident", "zi0", "zi1", "zi2"], "k7")

        win = T.xi[:, 0:W] if r == 0 else buf[:, XO:XO + W]
        wr_ = (xin if r == 0 else xr) + ["g%d" % r]

        def plus(a):
            own, ow = (buf[:, XO + a:XO + V:4], xr) if r == 0 else (T.xc[:, CH * a:CH * (a + 1)], ["xc%d" % a])
            tt(buf[:, a:V:4], win.indirect(T.og[:, 28 * a:28 * a + 28]), own, A.add, wr_ + ow + ["og%d" % (a // 2)], ["sp%d" % a])
            act(T.absp[:, CH * a:CH * (a + 1)], buf[:, a:V:4], FN.Abs, ["sp%d" % a], ["ap%d" % a])
            for b in range(4):
                mm(L[0:NC, a + 4 * b:128:16], T.absp[:, CH * a + b:CH * (a + 1):4], T.b16[:, 0:8], True, True, ["ap%d" % a], "k4")

        def minus(a, h=None):
            if h is None:
                src, sp, sm, ab, bs, nm = (X2[a][:, 0:CH], buf[:, a:V:4], buf[:, V + a:XO:4],
                                           T.absm[:, CH * a:CH * (a + 1)], (0, 1, 2, 3), str(a))
            else:
                src, sp, sm, ab, bs, nm = (X2[a][:, h:CH:2], buf[:, a + 4 * h:V:8], buf[:, V + a + 4 * h:XO:8],
                                           T.absm[:, CH * a + h:CH * (a + 1):2], (h, h + 2), str(a) + "ab"[h])
            tt(sm, src, sp, A.subtract, ["sp%d" % a], ["sm" + nm], ["k%d" % a])
            act(ab, sm, FN.Abs, ["sm" + nm], ["am" + nm])
            for b in bs:
                mm(L[0:NC, 128 + a + 4 * b:256:16], T.absm[:, CH * a + b:CH * (a + 1):4], T.b16[:, 0:8], True, True, ["am" + nm], "k4")

        plus(0)
        plus(1)
        minus(0)
        plus(2)
        minus(1)
        plus(3)
        minus(2)
        minus(3, 0)
        minus(3, 1)
        tt(T.tt[:], T.pws[:], T.vws[:], A.subtract, ["pws", "vws"], ["tt"])

        tt(T.f1[0:NC, :], L[0:NC, 0:256], T.old[0:NC, :], A.is_lt, ["olda", "oldb"], ["f1"], ["k4"])
        tt(T.f[0:NC, :], L[0:NC, 0:256], T.f1[0:NC, :], A.min, ["f1"], ["f"], ["k4"])
        src = buf[:, 0:XO + V]
        sr = xr + ["sp0", "sp1", "sp2", "sp3", "sm0", "sm1", "sm2", "sm3a", "sm3b", "uo"]

        def places():
            mm(L[:, 256:256 + NC], T.f[0:NC + 1, 0:128], T.ra[0:NC + 1, :], True, False, ["f", "ra"], "k4")
            mm(L[:, 256:256 + NC], T.f[0:NC, 128:256], T.rb[0:NC, :], False, True, ["f", "rb"], "k4")

        def places16():
            ts(T.uo[:], L[:, 256:256 + NC], UPD, None, A.add, None, ["upd"], ["uo"], ["k4"])

        def update(e, out, at, c0, c1, name):
            move(e, out[:, at + 16 * c0:at + 16 * c1], src.indirect(T.uo[:, c0:c1]), sr, [name])

        def follow(e, c0, c1, name):
            move(e, pws[r + 1][:, 16 * c0:16 * c1], pws[r][:, 0:W].indirect(T.qo[:, c0:c1]), pr + ["qo"], [name])

        if last:
            places()
            mm(S1[:, 0:NC], T.f[0:NC, 0:128], T.rm[0:NC, 1:224:2], True, False, ["f"] + RM, "k5")
            mm(S1[:, 0:NC], T.f[0:NC, 128:256], T.rm[0:NC, 1:224:2], False, True, ["f"] + RM, "k5")
            places16()
            for j, e in enumerate("vsvs"):
                update(e, T.xo, 0, 28 * j, 28 * j + 28, "xo%d" % j)
                dma("y", T.yx[:, CH * j:CH * (j + 1)], T.xo[:, CH * j:CH * (j + 1)], ["xo%d" % j])
                if j == 0:
                    tt(T.qt[:], S1[:, 0:NC], T.tt[:], A.mult, ["tt"], ["qt"], ["k5"])
                    tt(T.qq[:], T.qt[:], T.pwf[:], A.add, ["qt", "pwf"], ["qq"])
                    cp(T.qo[:], T.qq[:], ["qq"], ["qo"])
            follow("v", 0, 48, "p3a")
            follow("s", 48, NC, "p3b")
            for l in range(16):
                rr = (["p3a"] if l <= 6 else []) + (["p3b"] if l >= 6 else [])
                mm(PB[:, 0:NC], E[l], T.pw3[:, NC * l:NC * (l + 1)], l == 0, l == 15, rr, "k6")
            ts(T.ycb[:], PB[:, 0:NC], float(-K0), None, A.add, None, (), ["ycb"], ["k6"])
            dma("y", T.yc[:], T.ycb[:], ["ycb"])
            break

        nxt, zw, gb, hm = bufs[r + 1], (T.zw0, T.zw1)[r], (T.gb0, T.gb1)[r], (T.hm0, T.hm1)[r]
        mm(S1[:, 0:288], T.f[0:NC, 0:128], T.rm[0:NC, :], True, False, ["f"] + RM, "k5")
        mm(S1[:, 0:288], T.f[0:NC, 128:256], T.rm[0:NC, :], False, True, ["f"] + RM, "k5")
        places()
        cp(T.ev[:], S1[:, 0:288], (), ["ev"], ["k5"])
        places16()
        mm(PB[:, 0:288], T.blk[:], T.ev[:], False, True, ["blk", "ev"], "k6")
        mm(ZB[:, 0:NS], T.lt[:], T.ev[:, 1:288:2], False, True, ["lt", "ev"], "k7")
        na, nb = "x%da" % (r + 1), "x%db" % (r + 1)
        update("s", nxt, XO, 0, 24, na)
        op("v", lambda q: q.tensor_tensor_scan(T.sc[:], T.rst[:], PB[:, 0:288], 0.0, A.min, A.max), ["rst"], ["sc"], ["k6"])
        act(T.zv[:], ZB[:, 0:NS], FN.Identity, (), ["zv"], ["k7"], scale=1.0 / 64)
        update("s", nxt, XO, 24, NC, nb)
        ts(T.so[:, 0:9], T.sc[:, 31:288:32], -BIG, None, A.add, None, ["sc"], ["so"])
        zr = ["zz%d" % r, "zs%d" % r]
        cp(zw[:, 0:ZW].indirect(T.so[:, 0:9]), T.zv[:], ["so", "zv"], zr)
        op("v", lambda q: q.tensor_tensor_scan(hm[:], zw[:, STEP:STEP + G], zw[:, 0:G], -1000.0, A.add, A.max), zr, ["hm%d" % r])
        for l in range(16):
            mm(S1[:, 0:24], E[l], hm[:, l:G:16], l == 0, l == 15, ["hm%d" % r], "k5")
        tt(T.qt[:], T.ev[:, 1:224:2], T.tt[:], A.mult, ["ev", "tt"], ["qt"])
        tt(T.qq[:], T.qt[:], T.pwf[:], A.add, ["qt", "pwf"], ["qq"])
        ts(T.ho[:, 0:24], S1[:, 0:24], float(-K0), None, A.add, None, (), ["ho"], ["k5"])
        xr = [na, nb]
        for h, e in enumerate("vs"):
            move(e, gb[:, 192 * h:192 * h + 192], nxt[:, XO:XO + V].indirect(T.ho[:, 12 * h:12 * h + 12]), xr + ["ho"], ["gb%d%d" % (r, h)])
        spread(gb[:], nxt, XO + V, "ar%d" % (r + 1), ["gb%d0" % r, "gb%d1" % r], "g%d" % (r + 1))
        spread(hm[:], pws[r + 1], V, "ah%d" % (r + 1), ["hm%d" % r], "h%d" % (r + 1))

        cp(T.qo[:], T.qq[:], ["qq"], ["qo"])
        pa, pb_ = "p%da" % (r + 1), "p%db" % (r + 1)
        act(T.ot[0:NC, :], T.f[0:NC, :], FN.Identity, ["f"], ["ot"], bias=2.0 ** 25, scale=-2.0 ** 25)
        follow("v", 0, 48, pa)
        follow("s", 48, NC, pb_)
        tt(T.ou[0:NC, :], L[0:NC, 0:256], T.ot[0:NC, :], A.add, ["ot"], ["ou"], ["k4"])
        move("v", T.xc[:, 0:CH], nxt[:, XO:XO + V:4], xr, ["xc0"])
        tt(T.ov[0:NC, :], T.ou[0:NC, 0:128], T.ou[0:NC, 128:256], A.min, ["ou"], ["ov"])
        move("v", T.xc[:, CH:2 * CH], nxt[:, XO + 1:XO + V:4], xr, ["xc1"])
        tt(T.old[0:NC, 0:128], T.ov[0:NC, :], T.old[0:NC, 128:256], A.min, ["ov", "oldb"], ["olda"])
        move("v", T.xc[:, 2 * CH:3 * CH], nxt[:, XO + 2:XO + V:4], xr, ["xc2"])
        cp(T.old[0:NC, 128:256], T.old[0:NC, 0:128], ["olda"], ["oldb"])
        offsets(r + 1, [pa, pb_])
        twice(r + 1, xr)
        move("s", T.xc[:, 3 * CH:V], nxt[:, XO + 3:XO + V:4], xr, ["xc3"])
        pr = [pa, pb_, "h%d" % (r + 1)]

    for s, c in total.items():
        g.wait_ge(T.sem[s], c)
